import numpy as np
import ml_dtypes


def mxq(x, axis, fmt="e4m3"):
    dtype, down = {"e4m3": (ml_dtypes.float8_e4m3fn, 7), "e5m2": (ml_dtypes.float8_e5m2, 14)}[fmt]
    v = np.moveaxis(np.asarray(x, np.float32).astype(ml_dtypes.bfloat16).astype(np.float64), axis, -1)
    blocks = v.reshape(v.shape[:-1] + (-1, 32))
    amax = np.abs(blocks).max(-1, keepdims=True)
    byte = np.maximum(np.where(amax > 0, np.frexp(amax)[1] - 1 + 127, 0) - down, 1)
    scale = np.exp2(byte - 127.0)
    codes = (blocks / scale).astype(np.float32).astype(dtype).astype(np.float64)
    return np.moveaxis((codes * scale).reshape(v.shape), -1, axis)


WIDE = False


def mx_kscale(k):
    if not WIDE:
        return np.ones(k)
    levels = np.array([30, -30])
    if k % 512:
        return np.exp2(np.random.permutation(np.resize(levels, k // 32))).repeat(32)
    a = np.empty((k // 512, 16))
    for p in range(k // 512):
        a[p, :8] = np.random.permutation(np.resize(levels, 8))
        for g in range(8):
            far = levels[np.abs(levels - a[p, g]) >= 10]
            a[p, g + 8] = far[np.random.randint(len(far))]
    return np.exp2(a.ravel()).repeat(32)


BF16 = ml_dtypes.bfloat16


def bf(x):
    return np.asarray(x, np.float32).astype(BF16)


def f64(x):
    return np.asarray(x).astype(np.float64)


T, C, D, N = 2048, 1024, 1024, 1536


def setup_inputs():
    s, u = mx_kscale(T)[:, None], mx_kscale(C)[:, None]
    tail = np.exp(0.5 * np.random.standard_normal((T, N)))
    return {
        "x": bf(np.random.standard_normal((T, D)) * s),
        "dy": bf(np.random.standard_normal((T, N)) * tail / np.sqrt(T) / s),
        "c": bf(np.random.standard_normal((C, D)) * u),
        "e": bf(np.random.standard_normal((C, N)) / np.sqrt(C) / u),
        "resid": bf(np.random.uniform(-0.5, 0.5, (D, N))),
        "gscale": bf((1 + 0.1 * np.random.standard_normal(N)) / np.sqrt(D)),
    }


def reference(x, dy, c, e, resid, gscale):
    xq = mxq(f64(x), 0, "e4m3")
    dyq = mxq(f64(dy), 0, "e5m2")
    cq = mxq(f64(c), 0, "e4m3")
    eq = mxq(f64(e), 0, "e4m3")
    g = (xq.T @ dyq) + (cq.T @ eq)
    dstep = (g * f64(resid)).sum(axis=0)
    return dstep * f64(gscale)

@@ -1,0 +1,242 @@
+from contextlib import ExitStack
+
+import concourse.mybir as mybir
+from concourse.masks import make_identity
+
+T, C, D, N = 2048, 1024, 1024, 1536
+FLOPS = 2 * (T + C) * D * N + 2 * D * N
+
+F32 = mybir.dt.float32
+BF16 = mybir.dt.bfloat16
+U32 = mybir.dt.uint32
+U8 = mybir.dt.uint8
+E4M3 = mybir.dt.float8_e4m3fn_x4
+E5M2 = mybir.dt.float8_e5m2_x4
+ALU = mybir.AluOpType
+
+P = 128
+PACK = 4
+K_PASS = P * PACK
+W = 512
+HALF = 256
+PASSES = (T + C) // K_PASS
+T_PASSES = T // K_PASS
+MX_BANKS = 6
+RAW_BUFS = 18
+GROUPED_BUFS = 4
+
+PIECES = (
+    [(side, 0, k) for k in range(PASSES) for side in ("d", "n")]
+    + [("n", 1, k) for k in range(PASSES)]
+    + [("d", 1, k) for k in range(PASSES)]
+    + [("n", 2, k) for k in range(PASSES)]
+)
+GROUPS = [(2 * nch + j, e, dch) for nch, dch in ((0, 0), (1, 0), (0, 1), (1, 1)) for j in range(2) for e in range(2)] + [
+    (blk, e, dch) for blk in (4, 5) for dch in range(2) for e in range(2)
+]
+RESID = [(0, 0), (1, 0), (0, 1), (1, 1), (2, 0), (2, 1)]
+RESID_LOAD_AFTER = [9,13,17,26,29,29]
+RESID_TURN_STEP = [11,15,19,28,30,31]
+PE_BUDGET = 7
+
+
+def vector_share(step):
+    return 256 if step < 19 else 192
+
+
+def epilogues_per_step(step):
+    return 1
+
+
+def tile_learned_step_gradient_s2_kernel(tc, x, dy, c, e, resid, gscale, out):
+    nc = tc.nc
+    n_pieces = len(PIECES)
+
+    with ExitStack() as ctx:
+        keep = ctx.enter_context(tc.tile_pool(name="keep", bufs=1))
+        rawp = ctx.enter_context(tc.tile_pool(name="rawp", bufs=RAW_BUFS))
+        grp = ctx.enter_context(tc.tile_pool(name="grp", bufs=GROUPED_BUFS))
+        rrawp = ctx.enter_context(tc.tile_pool(name="rrawp", bufs=3))
+        junkp = ctx.enter_context(tc.tile_pool(name="junkp", bufs=2))
+        psum = ctx.enter_context(tc.psum_pool(name="psum", bufs=1))
+        ctx.enter_context(tc.manual_schedule())
+
+        codes = keep.tile([P, n_pieces, W], U32, align_bytes=256)
+        scales = keep.tile([P, n_pieces, W], U8, align_bytes=256)
+        resid_t = keep.tile([P, N // HALF, D // W, W], F32)
+        part = keep.tile([P, 4, P], F32)
+        ident = keep.tile([P, P], F32)
+        gs = keep.tile([N // HALF, HALF], BF16)
+        res = keep.tile([N // HALF, HALF], F32)
+
+        nc.scalar.dma_start(out=gs[:], in_=gscale.rearrange("(j c) -> j c", c=HALF))
+        make_identity(nc, ident[:])
+        nc.gpsimd.memset(part[:], 0.0)
+
+        raw = {}
+        rraw = {}
+        grouped = {}
+        bank_tile = {}
+        index = {pc: s for s, pc in enumerate(PIECES)}
+
+        def load(s):
+            side, ch, k = PIECES[s]
+            if k < T_PASSES:
+                src, k0 = (x if side == "d" else dy), k * K_PASS
+            else:
+                src, k0 = (c if side == "d" else e), (k - T_PASSES) * K_PASS
+            raw[s] = rawp.tile([P, PACK, W], BF16, name="raw")
+            nc.sync.dma_start(
+                out=raw[s][:],
+                in_=src[k0 : k0 + K_PASS, ch * W : (ch + 1) * W].rearrange("(p j) w -> p j w", j=PACK),
+            )
+            for r, after in enumerate(RESID_LOAD_AFTER):
+                if after == s:
+                    nch, dch = RESID[r]
+                    rraw[r] = rrawp.tile([P, 4, W], BF16, name="rraw")
+                    nc.sync.dma_start(
+                        out=rraw[r][:],
+                        in_=resid[dch * W : (dch + 1) * W, nch * W : (nch + 1) * W].rearrange("(t p) n -> p t n", p=P),
+                    )
+
+        def interleave_cols(copy, s, lo, hi):
+            src, dst = raw[s], grouped[s]
+            if PIECES[s][0] == "d":
+                copy(
+                    out=dst[:, lo * PACK : hi * PACK].rearrange("p (c i t) -> p c t i", i=4, t=PACK),
+                    in_=src[:, :, lo:hi].rearrange("p t (c i) -> p c t i", i=4),
+                )
+            else:
+                for h in range(2):
+                    a, b = max(lo, h * HALF), min(hi, (h + 1) * HALF)
+                    if a < b:
+                        blk = dst[:, h * HALF * PACK : (h + 1) * HALF * PACK].rearrange("p (e q t) -> p e q t", e=2, t=PACK)
+                        qa, qb = (a - h * HALF) // 2, (b - h * HALF) // 2
+                        copy(
+                            out=blk[:, :, qa:qb, :].rearrange("p e (c i) t -> p c t i e", i=2),
+                            in_=src[:, :, a:b].rearrange("p t (c i e) -> p c t i e", i=2, e=2),
+                        )
+
+        def interleave(s):
+            grouped[s] = grp.tile([P, W * PACK], BF16, name="grouped", align_bytes=256)
+            share = vector_share(s)
+            if share:
+                interleave_cols(nc.vector.tensor_copy, s, 0, share)
+            interleave_cols(nc.scalar.copy, s, share, W)
+
+        def fmt(s):
+            side, ch, k = PIECES[s]
+            return E5M2 if side == "n" and k < T_PASSES else E4M3
+
+        def quantize(s):
+            nc.vector.quantize_mx(out=codes[:, s, :].bitcast(fmt(s)), scales=scales[:, s, :], in_=grouped[s][:])
+
+        def turn_resid(r):
+            nch, dch = RESID[r]
+            words = rraw[r][:].rearrange("p t n -> p (t n)").bitcast(F32)
+            for h in range(2):
+                bank = psum.tile([P, W], F32, name="turn%d" % h)
+                for t in range(4):
+                    nc.tensor.transpose(bank[:, t * P : (t + 1) * P], words[:, t * HALF + h * P : t * HALF + (h + 1) * P], ident[:])
+                nc.scalar.copy(out=resid_t[:, 2 * nch + h, dch, :], in_=bank[:])
+
+        def multiply(g, k, b):
+            blk, par, dch = g
+            if k == 0:
+                bank_tile[g] = psum.tile([P, W], F32, name="acc%d" % b)
+            sn, sd = index[("n", blk // 2, k)], index[("d", dch, k)]
+            cols = slice((blk % 2) * HALF + par * P, (blk % 2) * HALF + (par + 1) * P)
+            nc.tensor.matmul_mx(
+                out=bank_tile[g][:],
+                lhsT=codes[:, sn, cols].bitcast(fmt(sn)),
+                lhsT_scale=scales[:, sn, cols],
+                rhs=codes[:, sd, :].bitcast(E4M3),
+                rhs_scale=scales[:, sd, :],
+                start=(k == 0),
+                stop=(k == PASSES - 1),
+            )
+
+        def epilogue(g):
+            blk, par, dch = g
+            junk = junkp.tile([P, W], F32, name="junk")
+            nc.vector.scalar_tensor_tensor(
+                out=junk[:],
+                in0=bank_tile[g][:],
+                scalar=1.0,
+                in1=resid_t[:, blk, dch, :].bitcast(BF16)[:, par::2],
+                op0=ALU.mult,
+                op1=ALU.mult,
+                accum_out=part[:, 2 * par + dch, blk : blk + 1],
+            )
+
+        for s in range(RAW_BUFS):
+            load(s)
+        interleave(0)
+
+        ready = set()
+        turned = set()
+        nxt = {g: 0 for g in GROUPS}
+        opened, pending, free, bank_of = [], [], list(range(MX_BANKS)), {}
+        waiting = list(GROUPS)
+        finished = 0
+        step = 0
+        while finished < len(GROUPS):
+            if step + 1 < n_pieces:
+                interleave(step + 1)
+            if step + RAW_BUFS < n_pieces:
+                load(step + RAW_BUFS)
+            if step < n_pieces:
+                quantize(step)
+                ready.add(PIECES[step])
+            count = 0
+            while pending and count < epilogues_per_step(step) and pending[0][1] < step and (pending[0][0][0] // 2, pending[0][0][2]) in turned:
+                g = pending.pop(0)[0]
+                epilogue(g)
+                free.append(bank_of[g])
+                count += 1
+                finished += 1
+            budget = PE_BUDGET
+            for r, when in enumerate(RESID_TURN_STEP):
+                if when == step:
+                    turn_resid(r)
+                    turned.add(RESID[r])
+                    budget -= 3
+            while budget > 0:
+                can = [g for g in opened if ("d", g[2], nxt[g]) in ready and ("n", g[0] // 2, nxt[g]) in ready]
+                if not can and waiting and free and ("d", waiting[0][2], 0) in ready and ("n", waiting[0][0] // 2, 0) in ready:
+                    g = waiting.pop(0)
+                    bank_of[g] = free.pop(0)
+                    opened.append(g)
+                    can = [g]
+                if not can:
+                    break
+                g = can[0]
+                multiply(g, nxt[g], bank_of[g])
+                nxt[g] += 1
+                budget -= 1
+                if nxt[g] == PASSES:
+                    opened.remove(g)
+                    pending.append((g, step))
+            step += 1
+
+        fin = psum.tile([P, HALF], F32, name="turn0")
+        for par in range(2):
+            for dch in range(2):
+                nc.tensor.matmul(
+                    out=fin[:, par * P : (par + 1) * P],
+                    lhsT=part[:, 2 * par + dch, :],
+                    rhs=ident[:],
+                    start=(dch == 0),
+                    stop=(dch == 1),
+                    is_transpose=True,
+                )
+        rows = N // HALF
+        nc.vector.tensor_tensor(
+            out=res[:].rearrange("j (q e) -> j q e", e=2),
+            in0=fin[0:rows, :].rearrange("j (e q) -> j q e", e=2),
+            in1=gs[:].rearrange("j (q e) -> j q e", e=2),
+            op=ALU.mult,
+        )
+        view = out.rearrange("(j c) -> j c", c=HALF)
+        nc.sync.dma_start(out=view[0:4, :], in_=res[0:4, :])
+        nc.scalar.dma_start(out=view[4:6, :], in_=res[4:6, :])

@@ -17,35 +17,43 @@ ALU = mybir.AluOpType
 P = 128
 PACK = 4
 K_PASS = P * PACK
-W = 512
-HALF = 256
+CHUNK = 512
+BLOCK = 256
+RUN = 4
 PASSES = (T + C) // K_PASS
 T_PASSES = T // K_PASS
-MX_BANKS = 6
-RAW_BUFS = 18
-GROUPED_BUFS = 4
+N_BLOCKS = N // BLOCK
+D_CHUNKS = D // CHUNK
+BANKS = 8
 
+SPLIT_PASSES = 3
 PIECES = (
-    [(side, 0, k) for k in range(PASSES) for side in ("d", "n")]
-    + [("n", 1, k) for k in range(PASSES)]
-    + [("d", 1, k) for k in range(PASSES)]
-    + [("n", 2, k) for k in range(PASSES)]
+    [piece for k in range(PASSES - SPLIT_PASSES) for piece in (("d", 0, 2, k), ("n", 0, 1, k))]
+    + [piece for k in range(PASSES - SPLIT_PASSES, PASSES) for piece in (("d", 0, 1, k), ("n", 0, 1, k), ("d", 1, 1, k))]
+    + [("n", chunk, 1, k) for chunk in (1, 2) for k in range(PASSES)]
 )
-GROUPS = [(2 * nch + j, e, dch) for nch, dch in ((0, 0), (1, 0), (0, 1), (1, 1)) for j in range(2) for e in range(2)] + [
-    (blk, e, dch) for blk in (4, 5) for dch in range(2) for e in range(2)
+GROUPS = [(blk, par, dch) for dch in range(D_CHUNKS) for blk in range(2) for par in range(2)] + [
+    (blk, par, dch) for blk in range(2, N_BLOCKS) for dch in range(D_CHUNKS) for par in range(2)
 ]
-RESID = [(0, 0), (1, 0), (0, 1), (1, 1), (2, 0), (2, 1)]
-RESID_LOAD_AFTER = [9,13,17,26,29,29]
-RESID_TURN_STEP = [11,15,19,28,30,31]
-PE_BUDGET = 7
+SQUARES = [(nch, dch) for nch in range(N // CHUNK) for dch in range(D_CHUNKS)]
+TURNS = [(blk, dch) for dch in range(D_CHUNKS) for blk in range(2)] + [
+    (blk, dch) for blk in range(2, N_BLOCKS) for dch in range(D_CHUNKS)
+]
 
+SQUARE_BEFORE_PIECE = [3, 16, 17, 17, 19, 26]
+TURN_STEP = [1, 1, 14, 14, 15, 15, 15, 16, 17, 27, 27, 27]
+CLOSE_BEFORE = {15: 2, 27: 2}
+CLOSE_AFTER = {14: 2, 16: 3}
+STEP_PASSES = 8
+STEP_PASSES_AT = {16: 12}
+TURN_COST = 1.5
+SCALAR_ONLY_PIECES = (15, 17, 23, 24, 26)
 
-def vector_share(step):
-    return 256 if step < 19 else 192
-
-
-def epilogues_per_step(step):
-    return 1
+LOAD_AHEAD = 7
+RAW_BUFS = {"d": 4, "n": 9}
+GROUPED_BUFS = {2: 2, 1: 5}
+SQUARE_BUFS = 4
+PRODUCT_BUFS = 2
 
 
 def tile_learned_step_gradient_s2_kernel(tc, x, dy, c, e, resid, gscale, out):
@@ -54,189 +62,205 @@ def tile_learned_step_gradient_s2_kernel(tc, x, dy, c, e, resid, gscale, out):
 
     with ExitStack() as ctx:
         keep = ctx.enter_context(tc.tile_pool(name="keep", bufs=1))
-        rawp = ctx.enter_context(tc.tile_pool(name="rawp", bufs=RAW_BUFS))
-        grp = ctx.enter_context(tc.tile_pool(name="grp", bufs=GROUPED_BUFS))
-        rrawp = ctx.enter_context(tc.tile_pool(name="rrawp", bufs=3))
-        junkp = ctx.enter_context(tc.tile_pool(name="junkp", bufs=2))
+        stream = ctx.enter_context(tc.tile_pool(name="stream", bufs=1))
         psum = ctx.enter_context(tc.psum_pool(name="psum", bufs=1))
         ctx.enter_context(tc.manual_schedule())
 
-        codes = keep.tile([P, n_pieces, W], U32, align_bytes=256)
-        scales = keep.tile([P, n_pieces, W], U8, align_bytes=256)
-        resid_t = keep.tile([P, N // HALF, D // W, W], F32)
-        part = keep.tile([P, 4, P], F32)
+        codes = [keep.tile([P, pc[2] * CHUNK], U32, name="codes%d" % s, align_bytes=256) for s, pc in enumerate(PIECES)]
+        scales = [keep.tile([P, pc[2] * CHUNK], U8, name="scales%d" % s, align_bytes=256) for s, pc in enumerate(PIECES)]
+        resid_t = keep.tile([P, N_BLOCKS, D_CHUNKS, CHUNK], F32)
+        sums = keep.tile([P, 2 * D_CHUNKS, P], F32)
         ident = keep.tile([P, P], F32)
-        gs = keep.tile([N // HALF, HALF], BF16)
-        res = keep.tile([N // HALF, HALF], F32)
+        gscale_rows = keep.tile([N_BLOCKS, BLOCK], BF16)
+        result = keep.tile([N_BLOCKS, BLOCK], F32)
 
-        nc.scalar.dma_start(out=gs[:], in_=gscale.rearrange("(j c) -> j c", c=HALF))
         make_identity(nc, ident[:])
-        nc.gpsimd.memset(part[:], 0.0)
+        nc.vector.memset(sums[:], 0.0)
 
-        raw = {}
-        rraw = {}
-        grouped = {}
-        bank_tile = {}
-        index = {pc: s for s, pc in enumerate(PIECES)}
+        raw, squares, grouped, group_bank = {}, {}, {}, {}
+        place = {
+            (side, first + i, k): (s, i * CHUNK) for s, (side, first, chunks, k) in enumerate(PIECES) for i in range(chunks)
+        }
+
+        def load_square(nch, dch):
+            squares[(nch, dch)] = stream.tile([P, CHUNK // P, CHUNK], BF16, name="square", bufs=SQUARE_BUFS)
+            nc.sync.dma_start(
+                out=squares[(nch, dch)][:],
+                in_=resid[dch * CHUNK : (dch + 1) * CHUNK, nch * CHUNK : (nch + 1) * CHUNK].rearrange("(t p) n -> p t n", p=P),
+            )
 
         def load(s):
-            side, ch, k = PIECES[s]
+            for square, before in zip(SQUARES, SQUARE_BEFORE_PIECE):
+                if before == s:
+                    load_square(*square)
+            side, first, chunks, k = PIECES[s]
+            if side == "d" and first > 0:
+                return
             if k < T_PASSES:
                 src, k0 = (x if side == "d" else dy), k * K_PASS
             else:
                 src, k0 = (c if side == "d" else e), (k - T_PASSES) * K_PASS
-            raw[s] = rawp.tile([P, PACK, W], BF16, name="raw")
+            width = D if side == "d" else CHUNK
+            tile = stream.tile([P, PACK, width], BF16, name="raw_" + side, bufs=RAW_BUFS[side])
             nc.sync.dma_start(
-                out=raw[s][:],
-                in_=src[k0 : k0 + K_PASS, ch * W : (ch + 1) * W].rearrange("(p j) w -> p j w", j=PACK),
+                out=tile[:],
+                in_=src[k0 : k0 + K_PASS, first * CHUNK : first * CHUNK + width].rearrange("(p t) w -> p t w", t=PACK),
             )
-            for r, after in enumerate(RESID_LOAD_AFTER):
-                if after == s:
-                    nch, dch = RESID[r]
-                    rraw[r] = rrawp.tile([P, 4, W], BF16, name="rraw")
-                    nc.sync.dma_start(
-                        out=rraw[r][:],
-                        in_=resid[dch * W : (dch + 1) * W, nch * W : (nch + 1) * W].rearrange("(t p) n -> p t n", p=P),
-                    )
+            for i in range(width // CHUNK):
+                raw[(side, first + i, k)] = (tile, i * CHUNK)
 
-        def interleave_cols(copy, s, lo, hi):
-            src, dst = raw[s], grouped[s]
-            if PIECES[s][0] == "d":
+        def interleave_columns(copy, s, lo, hi):
+            side, first, chunks, k = PIECES[s]
+            tile, col0 = raw[(side, first, k)]
+            if side == "d":
                 copy(
-                    out=dst[:, lo * PACK : hi * PACK].rearrange("p (c i t) -> p c t i", i=4, t=PACK),
-                    in_=src[:, :, lo:hi].rearrange("p t (c i) -> p c t i", i=4),
+                    out=grouped[s][:, lo * PACK : hi * PACK].rearrange("p (c i t) -> p c t i", i=RUN, t=PACK),
+                    in_=tile[:, :, col0 + lo : col0 + hi].rearrange("p t (c i) -> p c t i", i=RUN),
                 )
             else:
-                for h in range(2):
-                    a, b = max(lo, h * HALF), min(hi, (h + 1) * HALF)
-                    if a < b:
-                        blk = dst[:, h * HALF * PACK : (h + 1) * HALF * PACK].rearrange("p (e q t) -> p e q t", e=2, t=PACK)
-                        qa, qb = (a - h * HALF) // 2, (b - h * HALF) // 2
-                        copy(
-                            out=blk[:, :, qa:qb, :].rearrange("p e (c i) t -> p c t i e", i=2),
-                            in_=src[:, :, a:b].rearrange("p t (c i e) -> p c t i e", i=2, e=2),
-                        )
+                for b0 in range(lo, hi, BLOCK):
+                    copy(
+                        out=grouped[s][:, b0 * PACK : (b0 + BLOCK) * PACK].rearrange("p (e c i t) -> p e c t i", e=2, i=RUN, t=PACK),
+                        in_=tile[:, :, b0 : b0 + BLOCK].rearrange("p t (c i e) -> p e c t i", i=RUN, e=2),
+                    )
 
         def interleave(s):
-            grouped[s] = grp.tile([P, W * PACK], BF16, name="grouped", align_bytes=256)
-            share = vector_share(s)
-            if share:
-                interleave_cols(nc.vector.tensor_copy, s, 0, share)
-            interleave_cols(nc.scalar.copy, s, share, W)
+            chunks = PIECES[s][2]
+            width = chunks * CHUNK
+            grouped[s] = stream.tile([P, width * PACK], BF16, name="grouped%d" % chunks, bufs=GROUPED_BUFS[chunks], align_bytes=256)
+            vector_columns = 0 if s in SCALAR_ONLY_PIECES else width // 2
+            if vector_columns:
+                interleave_columns(nc.vector.tensor_copy, s, 0, vector_columns)
+            interleave_columns(nc.scalar.copy, s, vector_columns, width)
 
-        def fmt(s):
-            side, ch, k = PIECES[s]
+        def code_format(s):
+            side, first, chunks, k = PIECES[s]
             return E5M2 if side == "n" and k < T_PASSES else E4M3
 
         def quantize(s):
-            nc.vector.quantize_mx(out=codes[:, s, :].bitcast(fmt(s)), scales=scales[:, s, :], in_=grouped[s][:])
+            nc.vector.quantize_mx(out=codes[s][:].bitcast(code_format(s)), scales=scales[s][:], in_=grouped[s][:])
 
-        def turn_resid(r):
-            nch, dch = RESID[r]
-            words = rraw[r][:].rearrange("p t n -> p (t n)").bitcast(F32)
-            for h in range(2):
-                bank = psum.tile([P, W], F32, name="turn%d" % h)
-                for t in range(4):
-                    nc.tensor.transpose(bank[:, t * P : (t + 1) * P], words[:, t * HALF + h * P : t * HALF + (h + 1) * P], ident[:])
-                nc.scalar.copy(out=resid_t[:, 2 * nch + h, dch, :], in_=bank[:])
+        def turn(blk, dch, b):
+            words = squares[(blk // 2, dch)][:].rearrange("p t n -> p (t n)").bitcast(F32)
+            bank = psum.tile([P, CHUNK], F32, name="bank%d" % b)
+            for t in range(CHUNK // P):
+                w0 = t * (CHUNK // 2) + (blk % 2) * P
+                nc.tensor.transpose(bank[:, t * P : (t + 1) * P], words[:, w0 : w0 + P], ident[:])
+            nc.scalar.copy(out=resid_t[:, blk, dch, :], in_=bank[:])
 
-        def multiply(g, k, b):
-            blk, par, dch = g
+        def multiply(group, k, b):
+            blk, par, dch = group
             if k == 0:
-                bank_tile[g] = psum.tile([P, W], F32, name="acc%d" % b)
-            sn, sd = index[("n", blk // 2, k)], index[("d", dch, k)]
-            cols = slice((blk % 2) * HALF + par * P, (blk % 2) * HALF + (par + 1) * P)
+                group_bank[group] = psum.tile([P, CHUNK], F32, name="bank%d" % b)
+            sn, n0 = place[("n", blk // 2, k)]
+            sd, d0 = place[("d", dch, k)]
+            n0 += (blk % 2) * BLOCK + par * P
             nc.tensor.matmul_mx(
-                out=bank_tile[g][:],
-                lhsT=codes[:, sn, cols].bitcast(fmt(sn)),
-                lhsT_scale=scales[:, sn, cols],
-                rhs=codes[:, sd, :].bitcast(E4M3),
-                rhs_scale=scales[:, sd, :],
+                out=group_bank[group][:],
+                lhsT=codes[sn][:, n0 : n0 + P].bitcast(code_format(sn)),
+                lhsT_scale=scales[sn][:, n0 : n0 + P],
+                rhs=codes[sd][:, d0 : d0 + CHUNK].bitcast(E4M3),
+                rhs_scale=scales[sd][:, d0 : d0 + CHUNK],
                 start=(k == 0),
                 stop=(k == PASSES - 1),
             )
 
-        def epilogue(g):
-            blk, par, dch = g
-            junk = junkp.tile([P, W], F32, name="junk")
+        def close(group):
+            blk, par, dch = group
+            product = stream.tile([P, CHUNK], F32, name="product", bufs=PRODUCT_BUFS)
             nc.vector.scalar_tensor_tensor(
-                out=junk[:],
-                in0=bank_tile[g][:],
+                out=product[:],
+                in0=group_bank[group][:],
                 scalar=1.0,
                 in1=resid_t[:, blk, dch, :].bitcast(BF16)[:, par::2],
                 op0=ALU.mult,
                 op1=ALU.mult,
-                accum_out=part[:, 2 * par + dch, blk : blk + 1],
+                accum_out=sums[:, 2 * par + dch, blk : blk + 1],
             )
 
-        for s in range(RAW_BUFS):
+        quantised = set()
+        turned = set()
+        next_pass = {group: 0 for group in GROUPS}
+        waiting, running, finished, closed = list(GROUPS), [], [], []
+        free_banks, bank_of = list(range(BANKS)), {}
+        turns = list(zip(TURN_STEP, TURNS))
+
+        def can_run(group):
+            blk, par, dch = group
+            return ("d", dch, next_pass[group]) in quantised and ("n", blk // 2, next_pass[group]) in quantised
+
+        def close_groups(most):
+            for group in finished[:most]:
+                if (group[0], group[2]) not in turned:
+                    break
+                close(group)
+                finished.remove(group)
+                closed.append(group)
+                free_banks.append(bank_of[group])
+
+        for s in range(LOAD_AHEAD):
             load(s)
         interleave(0)
 
-        ready = set()
-        turned = set()
-        nxt = {g: 0 for g in GROUPS}
-        opened, pending, free, bank_of = [], [], list(range(MX_BANKS)), {}
-        waiting = list(GROUPS)
-        finished = 0
         step = 0
-        while finished < len(GROUPS):
+        while len(closed) < len(GROUPS):
             if step + 1 < n_pieces:
                 interleave(step + 1)
-            if step + RAW_BUFS < n_pieces:
-                load(step + RAW_BUFS)
+            if step + LOAD_AHEAD < n_pieces:
+                load(step + LOAD_AHEAD)
+            if step + LOAD_AHEAD == n_pieces:
+                nc.sync.dma_start(out=gscale_rows[:], in_=gscale.rearrange("(b j) -> b j", j=BLOCK))
+            close_groups(CLOSE_BEFORE.get(step, 0))
             if step < n_pieces:
                 quantize(step)
-                ready.add(PIECES[step])
-            count = 0
-            while pending and count < epilogues_per_step(step) and pending[0][1] < step and (pending[0][0][0] // 2, pending[0][0][2]) in turned:
-                g = pending.pop(0)[0]
-                epilogue(g)
-                free.append(bank_of[g])
-                count += 1
-                finished += 1
-            budget = PE_BUDGET
-            for r, when in enumerate(RESID_TURN_STEP):
-                if when == step:
-                    turn_resid(r)
-                    turned.add(RESID[r])
-                    budget -= 3
+                side, first, chunks, k = PIECES[step]
+                for i in range(chunks):
+                    quantised.add((side, first + i, k))
+            close_groups(CLOSE_AFTER.get(step, 1))
+
+            budget = STEP_PASSES_AT.get(step, STEP_PASSES)
+            turn_banks = []
+            while turns and turns[0][0] <= step and free_banks:
+                blk, dch = turns.pop(0)[1]
+                turn_banks.append(free_banks.pop(0))
+                turn(blk, dch, turn_banks[-1])
+                turned.add((blk, dch))
+                budget -= TURN_COST
             while budget > 0:
-                can = [g for g in opened if ("d", g[2], nxt[g]) in ready and ("n", g[0] // 2, nxt[g]) in ready]
-                if not can and waiting and free and ("d", waiting[0][2], 0) in ready and ("n", waiting[0][0] // 2, 0) in ready:
-                    g = waiting.pop(0)
-                    bank_of[g] = free.pop(0)
-                    opened.append(g)
-                    can = [g]
-                if not can:
+                ready = [group for group in running if can_run(group)]
+                if not ready and waiting and free_banks and can_run(waiting[0]):
+                    ready = [waiting.pop(0)]
+                    bank_of[ready[0]] = free_banks.pop(0)
+                    running.append(ready[0])
+                if not ready:
                     break
-                g = can[0]
-                multiply(g, nxt[g], bank_of[g])
-                nxt[g] += 1
+                group = ready[0]
+                multiply(group, next_pass[group], bank_of[group])
+                next_pass[group] += 1
                 budget -= 1
-                if nxt[g] == PASSES:
-                    opened.remove(g)
-                    pending.append((g, step))
+                if next_pass[group] == PASSES:
+                    running.remove(group)
+                    finished.append(group)
+            free_banks.extend(turn_banks)
             step += 1
 
-        fin = psum.tile([P, HALF], F32, name="turn0")
+        totals = psum.tile([P, BLOCK], F32, name="bank%d" % free_banks[0])
         for par in range(2):
-            for dch in range(2):
+            for dch in range(D_CHUNKS):
                 nc.tensor.matmul(
-                    out=fin[:, par * P : (par + 1) * P],
-                    lhsT=part[:, 2 * par + dch, :],
+                    out=totals[:, par * P : (par + 1) * P],
+                    lhsT=sums[:, 2 * par + dch, :],
                     rhs=ident[:],
                     start=(dch == 0),
-                    stop=(dch == 1),
+                    stop=(dch == D_CHUNKS - 1),
                     is_transpose=True,
                 )
-        rows = N // HALF
         nc.vector.tensor_tensor(
-            out=res[:].rearrange("j (q e) -> j q e", e=2),
-            in0=fin[0:rows, :].rearrange("j (e q) -> j q e", e=2),
-            in1=gs[:].rearrange("j (q e) -> j q e", e=2),
+            out=result[:].rearrange("b (q e) -> b q e", e=2),
+            in0=totals[0:N_BLOCKS, :].rearrange("b (e q) -> b q e", e=2),
+            in1=gscale_rows[:].rearrange("b (q e) -> b q e", e=2),
             op=ALU.mult,
         )
-        view = out.rearrange("(j c) -> j c", c=HALF)
-        nc.sync.dma_start(out=view[0:4, :], in_=res[0:4, :])
-        nc.scalar.dma_start(out=view[4:6, :], in_=res[4:6, :])
+        out_rows = out.rearrange("(b j) -> b j", j=BLOCK)
+        nc.sync.dma_start(out=out_rows[0:4, :], in_=result[0:4, :])
+        nc.scalar.dma_start(out=out_rows[4:N_BLOCKS, :], in_=result[4:N_BLOCKS, :])

from contextlib import ExitStack

import concourse.mybir as mybir
from concourse.masks import make_identity

T, C, D, N = 2048, 1024, 1024, 1536
FLOPS = 2 * (T + C) * D * N + 2 * D * N

F32 = mybir.dt.float32
BF16 = mybir.dt.bfloat16
U32 = mybir.dt.uint32
U8 = mybir.dt.uint8
E4M3 = mybir.dt.float8_e4m3fn_x4
E5M2 = mybir.dt.float8_e5m2_x4
ALU = mybir.AluOpType

P = 128
PACK = 4
K_PASS = P * PACK
CHUNK = 512
BLOCK = 256
RUN = 4
PASSES = (T + C) // K_PASS
T_PASSES = T // K_PASS
N_BLOCKS = N // BLOCK
D_CHUNKS = D // CHUNK
BANKS = 8

SPLIT_PASSES = 3
PIECES = (
    [piece for k in range(PASSES - SPLIT_PASSES) for piece in (("d", 0, 2, k), ("n", 0, 1, k))]
    + [piece for k in range(PASSES - SPLIT_PASSES, PASSES) for piece in (("d", 0, 1, k), ("n", 0, 1, k), ("d", 1, 1, k))]
    + [("n", chunk, 1, k) for chunk in (1, 2) for k in range(PASSES)]
)
GROUPS = [(blk, par, dch) for dch in range(D_CHUNKS) for blk in range(2) for par in range(2)] + [
    (blk, par, dch) for blk in range(2, N_BLOCKS) for dch in range(D_CHUNKS) for par in range(2)
]
SQUARES = [(nch, dch) for nch in range(N // CHUNK) for dch in range(D_CHUNKS)]
TURNS = [(blk, dch) for dch in range(D_CHUNKS) for blk in range(2)] + [
    (blk, dch) for blk in range(2, N_BLOCKS) for dch in range(D_CHUNKS)
]

SQUARE_BEFORE_PIECE = [3, 16, 17, 17, 19, 26]
TURN_STEP = [1, 1, 14, 14, 15, 15, 15, 16, 17, 27, 27, 27]
CLOSE_BEFORE = {15: 2, 27: 2}
CLOSE_AFTER = {14: 2, 16: 3}
STEP_PASSES = 8
STEP_PASSES_AT = {16: 12}
TURN_COST = 1.5
SCALAR_ONLY_PIECES = (15, 17, 23, 24, 26)

LOAD_AHEAD = 7
RAW_BUFS = {"d": 4, "n": 9}
GROUPED_BUFS = {2: 2, 1: 5}
SQUARE_BUFS = 4
PRODUCT_BUFS = 2


def tile_learned_step_gradient_s2_kernel(tc, x, dy, c, e, resid, gscale, out):
    nc = tc.nc
    n_pieces = len(PIECES)

    with ExitStack() as ctx:
        keep = ctx.enter_context(tc.tile_pool(name="keep", bufs=1))
        stream = ctx.enter_context(tc.tile_pool(name="stream", bufs=1))
        psum = ctx.enter_context(tc.psum_pool(name="psum", bufs=1))
        ctx.enter_context(tc.manual_schedule())

        codes = [keep.tile([P, pc[2] * CHUNK], U32, name="codes%d" % s, align_bytes=256) for s, pc in enumerate(PIECES)]
        scales = [keep.tile([P, pc[2] * CHUNK], U8, name="scales%d" % s, align_bytes=256) for s, pc in enumerate(PIECES)]
        resid_t = keep.tile([P, N_BLOCKS, D_CHUNKS, CHUNK], F32)
        sums = keep.tile([P, 2 * D_CHUNKS, P], F32)
        ident = keep.tile([P, P], F32)
        gscale_rows = keep.tile([N_BLOCKS, BLOCK], BF16)
        result = keep.tile([N_BLOCKS, BLOCK], F32)

        make_identity(nc, ident[:])
        nc.vector.memset(sums[:], 0.0)

        raw, squares, grouped, group_bank = {}, {}, {}, {}
        place = {
            (side, first + i, k): (s, i * CHUNK) for s, (side, first, chunks, k) in enumerate(PIECES) for i in range(chunks)
        }

        def load_square(nch, dch):
            squares[(nch, dch)] = stream.tile([P, CHUNK // P, CHUNK], BF16, name="square", bufs=SQUARE_BUFS)
            nc.sync.dma_start(
                out=squares[(nch, dch)][:],
                in_=resid[dch * CHUNK : (dch + 1) * CHUNK, nch * CHUNK : (nch + 1) * CHUNK].rearrange("(t p) n -> p t n", p=P),
            )

        def load(s):
            for square, before in zip(SQUARES, SQUARE_BEFORE_PIECE):
                if before == s:
                    load_square(*square)
            side, first, chunks, k = PIECES[s]
            if side == "d" and first > 0:
                return
            if k < T_PASSES:
                src, k0 = (x if side == "d" else dy), k * K_PASS
            else:
                src, k0 = (c if side == "d" else e), (k - T_PASSES) * K_PASS
            width = D if side == "d" else CHUNK
            tile = stream.tile([P, PACK, width], BF16, name="raw_" + side, bufs=RAW_BUFS[side])
            nc.sync.dma_start(
                out=tile[:],
                in_=src[k0 : k0 + K_PASS, first * CHUNK : first * CHUNK + width].rearrange("(p t) w -> p t w", t=PACK),
            )
            for i in range(width // CHUNK):
                raw[(side, first + i, k)] = (tile, i * CHUNK)

        def interleave_columns(copy, s, lo, hi):
            side, first, chunks, k = PIECES[s]
            tile, col0 = raw[(side, first, k)]
            if side == "d":
                copy(
                    out=grouped[s][:, lo * PACK : hi * PACK].rearrange("p (c i t) -> p c t i", i=RUN, t=PACK),
                    in_=tile[:, :, col0 + lo : col0 + hi].rearrange("p t (c i) -> p c t i", i=RUN),
                )
            else:
                for b0 in range(lo, hi, BLOCK):
                    copy(
                        out=grouped[s][:, b0 * PACK : (b0 + BLOCK) * PACK].rearrange("p (e c i t) -> p e c t i", e=2, i=RUN, t=PACK),
                        in_=tile[:, :, b0 : b0 + BLOCK].rearrange("p t (c i e) -> p e c t i", i=RUN, e=2),
                    )

        def interleave(s):
            chunks = PIECES[s][2]
            width = chunks * CHUNK
            grouped[s] = stream.tile([P, width * PACK], BF16, name="grouped%d" % chunks, bufs=GROUPED_BUFS[chunks], align_bytes=256)
            vector_columns = 0 if s in SCALAR_ONLY_PIECES else width // 2
            if vector_columns:
                interleave_columns(nc.vector.tensor_copy, s, 0, vector_columns)
            interleave_columns(nc.scalar.copy, s, vector_columns, width)

        def code_format(s):
            side, first, chunks, k = PIECES[s]
            return E5M2 if side == "n" and k < T_PASSES else E4M3

        def quantize(s):
            nc.vector.quantize_mx(out=codes[s][:].bitcast(code_format(s)), scales=scales[s][:], in_=grouped[s][:])

        def turn(blk, dch, b):
            words = squares[(blk // 2, dch)][:].rearrange("p t n -> p (t n)").bitcast(F32)
            bank = psum.tile([P, CHUNK], F32, name="bank%d" % b)
            for t in range(CHUNK // P):
                w0 = t * (CHUNK // 2) + (blk % 2) * P
                nc.tensor.transpose(bank[:, t * P : (t + 1) * P], words[:, w0 : w0 + P], ident[:])
            nc.scalar.copy(out=resid_t[:, blk, dch, :], in_=bank[:])

        def multiply(group, k, b):
            blk, par, dch = group
            if k == 0:
                group_bank[group] = psum.tile([P, CHUNK], F32, name="bank%d" % b)
            sn, n0 = place[("n", blk // 2, k)]
            sd, d0 = place[("d", dch, k)]
            n0 += (blk % 2) * BLOCK + par * P
            nc.tensor.matmul_mx(
                out=group_bank[group][:],
                lhsT=codes[sn][:, n0 : n0 + P].bitcast(code_format(sn)),
                lhsT_scale=scales[sn][:, n0 : n0 + P],
                rhs=codes[sd][:, d0 : d0 + CHUNK].bitcast(E4M3),
                rhs_scale=scales[sd][:, d0 : d0 + CHUNK],
                start=(k == 0),
                stop=(k == PASSES - 1),
            )

        def close(group):
            blk, par, dch = group
            product = stream.tile([P, CHUNK], F32, name="product", bufs=PRODUCT_BUFS)
            nc.vector.scalar_tensor_tensor(
                out=product[:],
                in0=group_bank[group][:],
                scalar=1.0,
                in1=resid_t[:, blk, dch, :].bitcast(BF16)[:, par::2],
                op0=ALU.mult,
                op1=ALU.mult,
                accum_out=sums[:, 2 * par + dch, blk : blk + 1],
            )

        quantised = set()
        turned = set()
        next_pass = {group: 0 for group in GROUPS}
        waiting, running, finished, closed = list(GROUPS), [], [], []
        free_banks, bank_of = list(range(BANKS)), {}
        turns = list(zip(TURN_STEP, TURNS))

        def can_run(group):
            blk, par, dch = group
            return ("d", dch, next_pass[group]) in quantised and ("n", blk // 2, next_pass[group]) in quantised

        def close_groups(most):
            for group in finished[:most]:
                if (group[0], group[2]) not in turned:
                    break
                close(group)
                finished.remove(group)
                closed.append(group)
                free_banks.append(bank_of[group])

        for s in range(LOAD_AHEAD):
            load(s)
        interleave(0)

        step = 0
        while len(closed) < len(GROUPS):
            if step + 1 < n_pieces:
                interleave(step + 1)
            if step + LOAD_AHEAD < n_pieces:
                load(step + LOAD_AHEAD)
            if step + LOAD_AHEAD == n_pieces:
                nc.sync.dma_start(out=gscale_rows[:], in_=gscale.rearrange("(b j) -> b j", j=BLOCK))
            close_groups(CLOSE_BEFORE.get(step, 0))
            if step < n_pieces:
                quantize(step)
                side, first, chunks, k = PIECES[step]
                for i in range(chunks):
                    quantised.add((side, first + i, k))
            close_groups(CLOSE_AFTER.get(step, 1))

            budget = STEP_PASSES_AT.get(step, STEP_PASSES)
            turn_banks = []
            while turns and turns[0][0] <= step and free_banks:
                blk, dch = turns.pop(0)[1]
                turn_banks.append(free_banks.pop(0))
                turn(blk, dch, turn_banks[-1])
                turned.add((blk, dch))
                budget -= TURN_COST
            while budget > 0:
                ready = [group for group in running if can_run(group)]
                if not ready and waiting and free_banks and can_run(waiting[0]):
                    ready = [waiting.pop(0)]
                    bank_of[ready[0]] = free_banks.pop(0)
                    running.append(ready[0])
                if not ready:
                    break
                group = ready[0]
                multiply(group, next_pass[group], bank_of[group])
                next_pass[group] += 1
                budget -= 1
                if next_pass[group] == PASSES:
                    running.remove(group)
                    finished.append(group)
            free_banks.extend(turn_banks)
            step += 1

        totals = psum.tile([P, BLOCK], F32, name="bank%d" % free_banks[0])
        for par in range(2):
            for dch in range(D_CHUNKS):
                nc.tensor.matmul(
                    out=totals[:, par * P : (par + 1) * P],
                    lhsT=sums[:, 2 * par + dch, :],
                    rhs=ident[:],
                    start=(dch == 0),
                    stop=(dch == D_CHUNKS - 1),
                    is_transpose=True,
                )
        nc.vector.tensor_tensor(
            out=result[:].rearrange("b (q e) -> b q e", e=2),
            in0=totals[0:N_BLOCKS, :].rearrange("b (e q) -> b q e", e=2),
            in1=gscale_rows[:].rearrange("b (q e) -> b q e", e=2),
            op=ALU.mult,
        )
        out_rows = out.rearrange("(b j) -> b j", j=BLOCK)
        nc.sync.dma_start(out=out_rows[0:4, :], in_=result[0:4, :])
        nc.scalar.dma_start(out=out_rows[4:N_BLOCKS, :], in_=result[4:N_BLOCKS, :])
